import numpy as np, ml_dtypes
CORES = [50,52,122,124]
N = 4
import mx_ref
NC, G = 192, 4
C = np.float32(0.041)
WID = [160,160,192,128]
BF = ml_dtypes.bfloat16
def cut(t, i, w=512):
    return t[:, w * i:w * i + w]
def tile(rs):
    return np.stack(rs, axis=2).reshape(128, -1).astype(BF)
def layer(w, X):
    out = []
    for i in range(G):
        for t in range(len(X)):
            p = mx_ref.matmul(mx_ref.quantize(cut(w, len(X) * i + t)), X[t])
            z = p if t == 0 else z + p
        out.append(z)
    return out
def act(Z):
    return [np.maximum(z, 0) * C for z in Z]
def setup_inputs(rng):
    def f(*shape):
        return mx_ref.flush((rng.standard_normal(shape, dtype=np.float32) * np.exp2(rng.integers(-2, 3, shape[:-1] + (1,)))).astype(BF))
    return {"x": f(N, 128, 4 * NC), "w1": f(N, 128, G * 512), "w2": f(N, 128, 512)}
def setup_inputs_blocks(rng):
    d = setup_inputs(rng)
    for k in ("x", "w1", "w2"): d[k] = mx_ref.spread(d[k], rng, 2)
    return d
def setup_inputs_wide(rng):
    d = setup_inputs(rng)
    for k in ("x", "w1", "w2"): d[k] = mx_ref.flush((d[k].astype(np.float32) * np.exp2(rng.integers(-6, 7, (N, 1, 1))).astype(np.float32)).astype(BF))
    return d
def reference(x, w1, w2):
    X = [mx_ref.quantize(x[j][:, :4 * WID[j]]) for j in range(N)]
    y = np.full((N, 128, NC), np.nan, np.float32)
    for c in range(N):
        for r in range(N):
            p = mx_ref.matmul(mx_ref.quantize(w2[r]), mx_ref.quantize(tile(act(layer(w1[r], [X[c]])))))
            z = p if r == 0 else z + p
        y[c][:, :WID[c]] = z
    return {"y": y}

@@ -1,0 +1,213 @@
+from concourse.mybir import dt, AluOpType, ActivationFunctionType
+
+WCOLS = 640
+XCOLS = 320
+NBANK = 6
+TCOL = [0, 128, 384, 512]
+W2COL = 256
+SCRATCH = {
+    "xb": ("sbuf", [128, 4 * 192], "bfloat16"),
+    "wb": ("sbuf", [128, 4 * WCOLS], "bfloat16"),
+    "xq": ("sbuf", [128, XCOLS], "float8_e4m3fn_x4"),
+    "xs": ("sbuf", [128, XCOLS], "uint8"),
+    "wq": ("sbuf", [128, WCOLS], "float8_e4m3fn_x4"),
+    "ws": ("sbuf", [128, WCOLS], "uint8"),
+    "fq": ("sbuf", [128, WCOLS], "float8_e4m3fn_x4"),
+    "fs": ("sbuf", [128, WCOLS], "uint8"),
+    "h": ("sbuf", [128, 4 * 2 * XCOLS], "bfloat16"),
+    "hq": ("sbuf", [128, 2 * XCOLS], "float8_e4m3fn_x4"),
+    "hs": ("sbuf", [128, 2 * XCOLS], "uint8"),
+    "ysend": ("sbuf", [128, 192], "float32"),
+    "yland": ("sbuf", [128, 192], "float32"),
+    "yout": ("sbuf", [128, 192], "float32"),
+    "z": ("psum", [128, 512 * NBANK], "float32"),
+    "yps": ("psum", [128, 512 * 2], "float32"),
+}
+SEMAPHORES = ["l0", "l1", "l2", "l3", "l4", "l5", "qin", "codesA", "codesB", "planes", "xarr", "yarr", "sent",
+              "mz", "ea", "ev", "qh", "my", "yc", "fin", "st"]
+
+
+def count(mask):
+    return bin(mask).count("1")
+
+
+def plan(T, topo):
+    cores, wid = T.cores, T.tables["WID"]
+    n = len(cores)
+    chip = [topo.chip(c) for c in cores]
+    partner = [[q for q in range(n) if q != r and chip[q] == chip[r]][0] for r in range(n)]
+    dest, relay = {}, {}
+    for r in range(n):
+        far = sorted([q for q in range(n) if chip[q] != chip[r]], key=lambda q: (-wid[q], q))
+        direct = topo.may_write(cores[r], cores[far[0]])
+        dest[r] = far[1] if direct else far[0]
+        if direct:
+            relay[r] = None
+        else:
+            d = cores[dest[r]]
+            able = [c for c in range(topo.CHIPS * topo.CORES_PER_CHIP)
+                    if topo.chip(c) == chip[r] and T.rank_of(c) is None and topo.may_write(c, d)]
+            near = [c for c in able if topo.die(c) == topo.die(cores[r])][0]
+            other = [c for c in able if topo.die(c) != topo.die(cores[r])][0]
+            relay[r] = (near, other)
+    return cores, wid, partner, dest, relay
+
+
+def rank_program(g, core, T, topo):
+    cores, wid, partner, dest, relay = plan(T, topo)
+    sem = T.sem
+    nsent = [0]
+
+    def send(dst, out, src, arrived, mask):
+        rid, pid, _ = topo.addr(dst)
+        g.remote_dma(out_ap=out, in_ap=src, remote_sem=arrived, local_sem=sem.sent, pid=pid, routing_id=rid, dma_engine_mask=mask)
+        nsent[0] += count(mask)
+
+    def codes(buf, a, b):
+        return buf[:, a:b].bitcast(dt.uint8)
+
+    cutcol = {r: (256 if relay[r] is None else 384) for r in dest}
+    far_core = [c for c in cores if topo.chip(c) != topo.chip(core)][0]
+    low = topo.mask(core, far_core)
+
+    rank = T.rank_of(core)
+    if rank is None:
+        for r in relay:
+            if relay[r] is None or core not in relay[r]:
+                continue
+            d, cut = cores[dest[r]], cutcol[r]
+            m = topo.mask(core, d)
+            if core == relay[r][0]:
+                g.wait_ge(sem.codesA, count(low))
+                send(d, codes(T.fq, 0, cut), codes(T.fq, 0, cut), sem.codesA, m)
+                g.wait_ge(sem.planes, count(low))
+                send(d, T.fs[:], T.fs[:], sem.planes, m)
+            else:
+                g.wait_ge(sem.codesB, count(topo.mask(cores[r], core) & ~low))
+                send(d, codes(T.fq, cut, WCOLS), codes(T.fq, cut, WCOLS), sem.codesB, m)
+            g.wait_ge(sem.sent, nsent[0])
+        return
+
+    mate = partner[rank]
+    po, pp = wid[rank], wid[mate]
+    pair = topo.mask(core, cores[mate])
+
+    def load(queue, s, out, in_):
+        queue.dma_start(out=out, in_=in_).then_inc(s, 16)
+
+    def tile_load(queue, s, t):
+        load(queue, s, T.wb[:, 4 * TCOL[t]:4 * TCOL[t] + 512], T.w1[:, 512 * t:512 * t + 512])
+
+    tile_load(g.sync, sem.l0, 0)
+    tile_load(g.scalar, sem.l1, 1)
+    load(g.sync, sem.l2, T.wb[:, 4 * W2COL:4 * W2COL + 512], T.w2[:])
+    tile_load(g.scalar, sem.l3, 2)
+    tile_load(g.sync, sem.l4, 3)
+    load(g.scalar, sem.l5, T.xb[:, 0:4 * po], T.x[:, 0:4 * po])
+
+    def quant_w(s, c):
+        g.vector.wait_ge(s, 16)
+        g.vector.quantize_mx(T.wq[:, c:c + 128], T.ws[:, c:c + 128], T.wb[:, 4 * c:4 * c + 512]).then_inc(sem.qin, 1)
+
+    quant_w(sem.l0, TCOL[0])
+    quant_w(sem.l1, TCOL[1])
+    quant_w(sem.l2, W2COL)
+    quant_w(sem.l3, TCOL[2])
+    quant_w(sem.l4, TCOL[3])
+    g.vector.wait_ge(sem.l5, 16)
+    g.vector.quantize_mx(T.xq[:, pp:pp + po], T.xs[:, pp:pp + po], T.xb[:, 0:4 * po]).then_inc(sem.qin, 1)
+
+    cut = cutcol[rank]
+    if relay[rank] is None:
+        d = cores[dest[rank]]
+        roads = [(d, topo.mask(core, d))] * 3
+    else:
+        near, other = relay[rank]
+        roads = [(near, low), (near, low), (other, topo.mask(core, other) & ~low)]
+    g.wait_ge(sem.qin, cut // 128)
+    send(roads[0][0], codes(T.fq, 0, cut), codes(T.wq, 0, cut), sem.codesA, roads[0][1])
+    g.wait_ge(sem.qin, 5)
+    send(roads[1][0], T.fs[:], T.ws[:], sem.planes, roads[1][1])
+    send(roads[2][0], codes(T.fq, cut, WCOLS), codes(T.wq, cut, WCOLS), sem.codesB, roads[2][1])
+    g.wait_ge(sem.qin, 6)
+    send(cores[mate], codes(T.xq, 0, po), codes(T.xq, pp, pp + po), sem.xarr, pair)
+    send(cores[mate], T.xs[:, 0:po], T.xs[:, pp:pp + po], sem.xarr, pair)
+    g.wait_ge(sem.yc, 1)
+    send(cores[mate], T.yland[:, 0:pp], T.ysend[:, 0:pp], sem.yarr, pair)
+    g.wait_ge(sem.sent, nsent[0])
+
+    blocks = [
+        (T.wq, T.ws, pp, po, 0, 0),
+        (T.wq, T.ws, 0, pp, po, 1),
+        (T.fq, T.fs, 0, pp, XCOLS, 1),
+        (T.fq, T.fs, pp, po, XCOLS + pp, 0),
+    ]
+    def evac_sem(k):
+        return (sem.ea if k % 2 == 0 else sem.ev), k // 2 + 1
+
+    def first(k):
+        wq, ws, xc, n, hc, yb = blocks[k // 4]
+        c, bank = TCOL[k % 4], 512 * (k % NBANK)
+        if k >= NBANK:
+            s, v = evac_sem(k - NBANK)
+            g.tensor.wait_ge(s, v)
+        g.tensor.matmul_mx(T.z[:, bank:bank + n], wq[:, c:c + 128], ws[:, c:c + 128], T.xq[:, xc:xc + n], T.xs[:, xc:xc + n],
+                           True, True).then_inc(sem.mz, 1)
+
+    def second(j):
+        wq, ws, xc, n, hc, yb = blocks[j]
+        g.tensor.wait_ge(sem.qh, j + 1)
+        g.tensor.matmul_mx(T.yps[:, 512 * yb:512 * yb + n], wq[:, W2COL:W2COL + 128], ws[:, W2COL:W2COL + 128],
+                           T.hq[:, hc:hc + n], T.hs[:, hc:hc + n], j < 2, j >= 2).then_inc(sem.my, 1)
+
+    g.tensor.wait_ge(sem.qin, 6)
+    for k in range(0, 4):
+        first(k)
+    g.tensor.wait_ge(sem.xarr, 2 * count(pair))
+    for k in range(4, 8):
+        first(k)
+    second(0)
+    second(1)
+    g.tensor.wait_ge(sem.codesA, count(low))
+    g.tensor.wait_ge(sem.planes, count(low))
+    first(8)
+    first(9)
+    g.tensor.wait_ge(sem.codesB, count(low))
+    for k in range(10, 14):
+        first(k)
+    second(2)
+    first(14)
+    first(15)
+    second(3)
+
+    def evac(k):
+        wq, ws, xc, n, hc, yb = blocks[k // 4]
+        b, bank = k % 4, 512 * (k % NBANK)
+        out, in_ = T.h[:, 4 * hc + b:4 * (hc + n):4], T.z[:, bank:bank + n]
+        if k % 2 == 0:
+            g.scalar.wait_ge(sem.mz, k + 1)
+            g.scalar.activation(out, in_, ActivationFunctionType.Relu, scale=0.041).then_inc(sem.ea, 1)
+        else:
+            g.vector.wait_ge(sem.mz, k + 1)
+            g.vector.tensor_scalar(out, in_, 0.0, 0.041, AluOpType.max, AluOpType.mult).then_inc(sem.ev, 1)
+
+    def quant_h(j):
+        wq, ws, xc, n, hc, yb = blocks[j]
+        g.vector.wait_ge(sem.ea, 2 * j + 2)
+        g.vector.wait_ge(sem.ev, 2 * j + 2)
+        g.vector.quantize_mx(T.hq[:, hc:hc + n], T.hs[:, hc:hc + n], T.h[:, 4 * hc:4 * (hc + n)]).then_inc(sem.qh, 1)
+
+    for j in range(4):
+        for b in range(4):
+            evac(4 * j + b)
+        quant_h(j)
+        if j == 2:
+            g.vector.wait_ge(sem.my, 3)
+            g.vector.tensor_copy(T.ysend[:, 0:pp], T.yps[:, 512:512 + pp]).then_inc(sem.yc, 1)
+
+    g.vector.wait_ge(sem.my, 4)
+    g.vector.wait_ge(sem.yarr, count(pair))
+    g.vector.tensor_tensor(T.yout[:, 0:po], T.yps[:, 0:po], T.yland[:, 0:po], AluOpType.add).then_inc(sem.fin, 1)
+    g.sync.wait_ge(sem.fin, 1)
+    g.sync.dma_start(out=T.y[:, 0:po], in_=T.yout[:, 0:po]).then_inc(sem.st, 16)
+    g.sync.wait_ge(sem.st, 16)

@@ -5,6 +5,12 @@ XCOLS = 320
 NBANK = 6
 TCOL = [0, 128, 384, 512]
 W2COL = 256
+DIRECT = [("c", 0, 256, None, "low"), ("c", 256, 384, "far", "low"), ("s", 0, 640, None, "low"), ("c", 384, 640, None, "low")]
+RELAYED = [("c", 0, 128, "near1", "low"), ("c", 128, 256, "near0", "high"), ("s", 0, 640, "near1", "low"),
+           ("c", 256, 384, "far", "low"), ("c", 384, 512, "mate", "high"), ("c", 512, 640, "near0", "low")]
+XPOS = {True: 3, False: 9}
+SEQ = [(0, 0), (0, 1), (0, 2), (0, 3), (1, 0), (1, 1), (1, 2), (1, 3), 0, (2, 0), 1, (2, 1), (2, 2), (2, 3), (3, 0), 2,
+       (3, 1), (3, 2), (3, 3), 3]
 SCRATCH = {
     "xb": ("sbuf", [128, 4 * 192], "bfloat16"),
     "wb": ("sbuf", [128, 4 * WCOLS], "bfloat16"),
@@ -14,6 +20,7 @@ SCRATCH = {
     "ws": ("sbuf", [128, WCOLS], "uint8"),
     "fq": ("sbuf", [128, WCOLS], "float8_e4m3fn_x4"),
     "fs": ("sbuf", [128, WCOLS], "uint8"),
+    "mq": ("sbuf", [128, WCOLS], "float8_e4m3fn_x4"),
     "h": ("sbuf", [128, 4 * 2 * XCOLS], "bfloat16"),
     "hq": ("sbuf", [128, 2 * XCOLS], "float8_e4m3fn_x4"),
     "hs": ("sbuf", [128, 2 * XCOLS], "uint8"),
@@ -23,8 +30,9 @@ SCRATCH = {
     "z": ("psum", [128, 512 * NBANK], "float32"),
     "yps": ("psum", [128, 512 * 2], "float32"),
 }
-SEMAPHORES = ["l0", "l1", "l2", "l3", "l4", "l5", "qin", "codesA", "codesB", "planes", "xarr", "yarr", "sent",
-              "mz", "ea", "ev", "qh", "my", "yc", "fin", "st"]
+NPIECE = max(len(DIRECT), len(RELAYED))
+SEMAPHORES = ["l0", "l1", "l2", "l3", "l5", "qin", "xarr", "yarr", "sent",
+              "mz", "ea", "ev", "qh", "my", "yc", "fin", "st"] + [a + str(i) for a in "pm" for i in range(NPIECE)]
 
 
 def count(mask):
@@ -36,25 +44,26 @@ def plan(T, topo):
     n = len(cores)
     chip = [topo.chip(c) for c in cores]
     partner = [[q for q in range(n) if q != r and chip[q] == chip[r]][0] for r in range(n)]
-    dest, relay = {}, {}
+    dest, pieces = {}, {}
     for r in range(n):
+        me = cores[r]
         far = sorted([q for q in range(n) if chip[q] != chip[r]], key=lambda q: (-wid[q], q))
-        direct = topo.may_write(cores[r], cores[far[0]])
+        direct = topo.may_write(me, cores[far[0]])
         dest[r] = far[1] if direct else far[0]
-        if direct:
-            relay[r] = None
-        else:
-            d = cores[dest[r]]
-            able = [c for c in range(topo.CHIPS * topo.CORES_PER_CHIP)
-                    if topo.chip(c) == chip[r] and T.rank_of(c) is None and topo.may_write(c, d)]
-            near = [c for c in able if topo.die(c) == topo.die(cores[r])][0]
-            other = [c for c in able if topo.die(c) != topo.die(cores[r])][0]
-            relay[r] = (near, other)
-    return cores, wid, partner, dest, relay
+        d = cores[dest[r]]
+        able = [c for c in range(topo.CHIPS * topo.CORES_PER_CHIP)
+                if T.rank_of(c) is None and topo.die(c) == topo.die(me) and topo.may_write(c, d)]
+        way = {"near%d" % i: c for i, c in enumerate([c for c in able if topo.chip(c) == chip[r]])}
+        way["far"] = [c for c in able if topo.mates(topo.chip(c), topo.chip(d)) and topo.same_plane(topo.chip(c), chip[r])][0]
+        way["mate"], way[None] = cores[partner[r]], None
+        full, low = topo.mask(me, cores[partner[r]]), topo.mask(me, d)
+        engines = {"low": low, "high": full & ~low}
+        pieces[r] = [(k, a, b, way[v], engines[m]) for k, a, b, v, m in (DIRECT if direct else RELAYED)]
+    return cores, wid, partner, dest, pieces
 
 
 def rank_program(g, core, T, topo):
-    cores, wid, partner, dest, relay = plan(T, topo)
+    cores, wid, partner, dest, pieces = plan(T, topo)
     sem = T.sem
     nsent = [0]
 
@@ -66,28 +75,26 @@ def rank_program(g, core, T, topo):
     def codes(buf, a, b):
         return buf[:, a:b].bitcast(dt.uint8)
 
-    cutcol = {r: (256 if relay[r] is None else 384) for r in dest}
-    far_core = [c for c in cores if topo.chip(c) != topo.chip(core)][0]
-    low = topo.mask(core, far_core)
+    def view(k, q, s, a, b):
+        return codes(q, a, b) if k == "c" else s[:, a:b]
+
+    def relay_for(r, q, arrived):
+        for i, (k, a, b, via, m) in enumerate(pieces[r]):
+            if via == core:
+                g.wait_ge(sem[arrived % i], count(m))
+                d = cores[dest[r]]
+                mask = topo.mask(core, d)
+                send(d, view(k, T.fq, T.fs, a, b), view(k, q, T.fs, a, b), sem["p%d" % i], mask)
 
     rank = T.rank_of(core)
     if rank is None:
-        for r in relay:
-            if relay[r] is None or core not in relay[r]:
-                continue
-            d, cut = cores[dest[r]], cutcol[r]
-            m = topo.mask(core, d)
-            if core == relay[r][0]:
-                g.wait_ge(sem.codesA, count(low))
-                send(d, codes(T.fq, 0, cut), codes(T.fq, 0, cut), sem.codesA, m)
-                g.wait_ge(sem.planes, count(low))
-                send(d, T.fs[:], T.fs[:], sem.planes, m)
-            else:
-                g.wait_ge(sem.codesB, count(topo.mask(cores[r], core) & ~low))
-                send(d, codes(T.fq, cut, WCOLS), codes(T.fq, cut, WCOLS), sem.codesB, m)
+        for r in pieces:
+            relay_for(r, T.fq, "p%d")
+        if nsent[0]:
             g.wait_ge(sem.sent, nsent[0])
         return
 
+    low = topo.mask(core, [c for c in cores if topo.chip(c) != topo.chip(core)][0])
     mate = partner[rank]
     po, pp = wid[rank], wid[mate]
     pair = topo.mask(core, cores[mate])
@@ -95,43 +102,46 @@ def rank_program(g, core, T, topo):
     def load(queue, s, out, in_):
         queue.dma_start(out=out, in_=in_).then_inc(s, 16)
 
-    def tile_load(queue, s, t):
-        load(queue, s, T.wb[:, 4 * TCOL[t]:4 * TCOL[t] + 512], T.w1[:, 512 * t:512 * t + 512])
-
-    tile_load(g.sync, sem.l0, 0)
-    tile_load(g.scalar, sem.l1, 1)
+    load(g.sync, sem.l0, T.wb[:, 0:256], T.w1[:, 0:256])
+    load(g.scalar, sem.l0, T.wb[:, 256:512], T.w1[:, 256:512])
     load(g.sync, sem.l2, T.wb[:, 4 * W2COL:4 * W2COL + 512], T.w2[:])
-    tile_load(g.scalar, sem.l3, 2)
-    tile_load(g.sync, sem.l4, 3)
+    load(g.scalar, sem.l1, T.wb[:, 512:1024], T.w1[:, 512:1024])
+    load(g.scalar, sem.l3, T.wb[:, 4 * TCOL[2]:4 * TCOL[2] + 1024], T.w1[:, 1024:2048])
     load(g.scalar, sem.l5, T.xb[:, 0:4 * po], T.x[:, 0:4 * po])
 
-    def quant_w(s, c):
-        g.vector.wait_ge(s, 16)
+    def quant_w(c):
         g.vector.quantize_mx(T.wq[:, c:c + 128], T.ws[:, c:c + 128], T.wb[:, 4 * c:4 * c + 512]).then_inc(sem.qin, 1)
 
-    quant_w(sem.l0, TCOL[0])
-    quant_w(sem.l1, TCOL[1])
-    quant_w(sem.l2, W2COL)
-    quant_w(sem.l3, TCOL[2])
-    quant_w(sem.l4, TCOL[3])
+    g.vector.wait_ge(sem.l0, 32)
+    quant_w(TCOL[0])
+    g.vector.wait_ge(sem.l1, 16)
+    quant_w(TCOL[1])
+    g.vector.wait_ge(sem.l2, 16)
+    quant_w(W2COL)
+    g.vector.wait_ge(sem.l3, 16)
+    quant_w(TCOL[2])
+    quant_w(TCOL[3])
     g.vector.wait_ge(sem.l5, 16)
     g.vector.quantize_mx(T.xq[:, pp:pp + po], T.xs[:, pp:pp + po], T.xb[:, 0:4 * po]).then_inc(sem.qin, 1)
 
-    cut = cutcol[rank]
-    if relay[rank] is None:
-        d = cores[dest[rank]]
-        roads = [(d, topo.mask(core, d))] * 3
-    else:
-        near, other = relay[rank]
-        roads = [(near, low), (near, low), (other, topo.mask(core, other) & ~low)]
-    g.wait_ge(sem.qin, cut // 128)
-    send(roads[0][0], codes(T.fq, 0, cut), codes(T.wq, 0, cut), sem.codesA, roads[0][1])
-    g.wait_ge(sem.qin, 5)
-    send(roads[1][0], T.fs[:], T.ws[:], sem.planes, roads[1][1])
-    send(roads[2][0], codes(T.fq, cut, WCOLS), codes(T.wq, cut, WCOLS), sem.codesB, roads[2][1])
-    g.wait_ge(sem.qin, 6)
-    send(cores[mate], codes(T.xq, 0, po), codes(T.xq, pp, pp + po), sem.xarr, pair)
-    send(cores[mate], T.xs[:, 0:po], T.xs[:, pp:pp + po], sem.xarr, pair)
+    xmask = pair & ~low
+
+    def send_tokens():
+        g.wait_ge(sem.qin, 6)
+        send(cores[mate], codes(T.xq, 0, po), codes(T.xq, pp, pp + po), sem.xarr, xmask)
+        send(cores[mate], T.xs[:, 0:po], T.xs[:, pp:pp + po], sem.xarr, xmask)
+
+    xpos = min(XPOS[topo.may_write(core, cores[dest[rank]])], len(pieces[rank]))
+    for i, (k, a, b, via, m) in enumerate(pieces[rank]):
+        if i == xpos:
+            send_tokens()
+        g.wait_ge(sem.qin, b // 128)
+        to_mate = via == cores[mate]
+        send(cores[dest[rank]] if via is None else via, view(k, T.mq if to_mate else T.fq, T.fs, a, b),
+             view(k, T.wq, T.ws, a, b), sem[("m%d" if to_mate else "p%d") % i], m)
+    if xpos == len(pieces[rank]):
+        send_tokens()
+    relay_for(mate, T.mq, "m%d")
     g.wait_ge(sem.yc, 1)
     send(cores[mate], T.yland[:, 0:pp], T.ysend[:, 0:pp], sem.yarr, pair)
     g.wait_ge(sem.sent, nsent[0])
@@ -142,15 +152,13 @@ def rank_program(g, core, T, topo):
         (T.fq, T.fs, 0, pp, XCOLS, 1),
         (T.fq, T.fs, pp, po, XCOLS + pp, 0),
     ]
-    def evac_sem(k):
-        return (sem.ea if k % 2 == 0 else sem.ev), k // 2 + 1
-
-    def first(k):
-        wq, ws, xc, n, hc, yb = blocks[k // 4]
-        c, bank = TCOL[k % 4], 512 * (k % NBANK)
+    def first(j, t):
+        wq, ws, xc, n, hc, yb = blocks[j]
+        k, c = 4 * j + t, TCOL[t]
+        bank = 512 * (k % NBANK)
         if k >= NBANK:
-            s, v = evac_sem(k - NBANK)
-            g.tensor.wait_ge(s, v)
+            o = k - NBANK
+            g.tensor.wait_ge(sem.ea if o % 2 == 0 else sem.ev, o // 2 + 1)
         g.tensor.matmul_mx(T.z[:, bank:bank + n], wq[:, c:c + 128], ws[:, c:c + 128], T.xq[:, xc:xc + n], T.xs[:, xc:xc + n],
                            True, True).then_inc(sem.mz, 1)
 
@@ -160,25 +168,28 @@ def rank_program(g, core, T, topo):
         g.tensor.matmul_mx(T.yps[:, 512 * yb:512 * yb + n], wq[:, W2COL:W2COL + 128], ws[:, W2COL:W2COL + 128],
                            T.hq[:, hc:hc + n], T.hs[:, hc:hc + n], j < 2, j >= 2).then_inc(sem.my, 1)
 
+    source = [r for r in dest if dest[r] == rank][0]
+    waited = []
+
+    def need(c):
+        for i, (k, a, b, via, m) in enumerate(pieces[source]):
+            if i not in waited and a < c + 128 and b > c:
+                waited.append(i)
+                last = cores[source] if via is None else via
+                g.tensor.wait_ge(sem["p%d" % i], count(topo.mask(last, core)))
+
     g.tensor.wait_ge(sem.qin, 6)
-    for k in range(0, 4):
-        first(k)
-    g.tensor.wait_ge(sem.xarr, 2 * count(pair))
-    for k in range(4, 8):
-        first(k)
-    second(0)
-    second(1)
-    g.tensor.wait_ge(sem.codesA, count(low))
-    g.tensor.wait_ge(sem.planes, count(low))
-    first(8)
-    first(9)
-    g.tensor.wait_ge(sem.codesB, count(low))
-    for k in range(10, 14):
-        first(k)
-    second(2)
-    first(14)
-    first(15)
-    second(3)
+    for e in SEQ:
+        if e == (1, 0):
+            g.tensor.wait_ge(sem.xarr, 2 * count(xmask))
+        if e in (0, 1, 2, 3):
+            if e == 2:
+                need(W2COL)
+            second(e)
+        else:
+            if e[0] >= 2:
+                need(TCOL[e[1]])
+            first(e[0], e[1])
 
     def evac(k):
         wq, ws, xc, n, hc, yb = blocks[k // 4]
@@ -191,16 +202,13 @@ def rank_program(g, core, T, topo):
             g.vector.wait_ge(sem.mz, k + 1)
             g.vector.tensor_scalar(out, in_, 0.0, 0.041, AluOpType.max, AluOpType.mult).then_inc(sem.ev, 1)
 
-    def quant_h(j):
+    for j in range(4):
         wq, ws, xc, n, hc, yb = blocks[j]
+        for b in range(4):
+            evac(4 * j + b)
         g.vector.wait_ge(sem.ea, 2 * j + 2)
         g.vector.wait_ge(sem.ev, 2 * j + 2)
         g.vector.quantize_mx(T.hq[:, hc:hc + n], T.hs[:, hc:hc + n], T.h[:, 4 * hc:4 * (hc + n)]).then_inc(sem.qh, 1)
-
-    for j in range(4):
-        for b in range(4):
-            evac(4 * j + b)
-        quant_h(j)
         if j == 2:
             g.vector.wait_ge(sem.my, 3)
             g.vector.tensor_copy(T.ysend[:, 0:pp], T.yps[:, 512:512 + pp]).then_inc(sem.yc, 1)

from concourse.mybir import dt, AluOpType, ActivationFunctionType

WCOLS = 640
XCOLS = 320
NBANK = 6
TCOL = [0, 128, 384, 512]
W2COL = 256
DIRECT = [("c", 0, 256, None, "low"), ("c", 256, 384, "far", "low"), ("s", 0, 640, None, "low"), ("c", 384, 640, None, "low")]
RELAYED = [("c", 0, 128, "near1", "low"), ("c", 128, 256, "near0", "high"), ("s", 0, 640, "near1", "low"),
           ("c", 256, 384, "far", "low"), ("c", 384, 512, "mate", "high"), ("c", 512, 640, "near0", "low")]
XPOS = {True: 3, False: 9}
SEQ = [(0, 0), (0, 1), (0, 2), (0, 3), (1, 0), (1, 1), (1, 2), (1, 3), 0, (2, 0), 1, (2, 1), (2, 2), (2, 3), (3, 0), 2,
       (3, 1), (3, 2), (3, 3), 3]
SCRATCH = {
    "xb": ("sbuf", [128, 4 * 192], "bfloat16"),
    "wb": ("sbuf", [128, 4 * WCOLS], "bfloat16"),
    "xq": ("sbuf", [128, XCOLS], "float8_e4m3fn_x4"),
    "xs": ("sbuf", [128, XCOLS], "uint8"),
    "wq": ("sbuf", [128, WCOLS], "float8_e4m3fn_x4"),
    "ws": ("sbuf", [128, WCOLS], "uint8"),
    "fq": ("sbuf", [128, WCOLS], "float8_e4m3fn_x4"),
    "fs": ("sbuf", [128, WCOLS], "uint8"),
    "mq": ("sbuf", [128, WCOLS], "float8_e4m3fn_x4"),
    "h": ("sbuf", [128, 4 * 2 * XCOLS], "bfloat16"),
    "hq": ("sbuf", [128, 2 * XCOLS], "float8_e4m3fn_x4"),
    "hs": ("sbuf", [128, 2 * XCOLS], "uint8"),
    "ysend": ("sbuf", [128, 192], "float32"),
    "yland": ("sbuf", [128, 192], "float32"),
    "yout": ("sbuf", [128, 192], "float32"),
    "z": ("psum", [128, 512 * NBANK], "float32"),
    "yps": ("psum", [128, 512 * 2], "float32"),
}
NPIECE = max(len(DIRECT), len(RELAYED))
SEMAPHORES = ["l0", "l1", "l2", "l3", "l5", "qin", "xarr", "yarr", "sent",
              "mz", "ea", "ev", "qh", "my", "yc", "fin", "st"] + [a + str(i) for a in "pm" for i in range(NPIECE)]


def count(mask):
    return bin(mask).count("1")


def plan(T, topo):
    cores, wid = T.cores, T.tables["WID"]
    n = len(cores)
    chip = [topo.chip(c) for c in cores]
    partner = [[q for q in range(n) if q != r and chip[q] == chip[r]][0] for r in range(n)]
    dest, pieces = {}, {}
    for r in range(n):
        me = cores[r]
        far = sorted([q for q in range(n) if chip[q] != chip[r]], key=lambda q: (-wid[q], q))
        direct = topo.may_write(me, cores[far[0]])
        dest[r] = far[1] if direct else far[0]
        d = cores[dest[r]]
        able = [c for c in range(topo.CHIPS * topo.CORES_PER_CHIP)
                if T.rank_of(c) is None and topo.die(c) == topo.die(me) and topo.may_write(c, d)]
        way = {"near%d" % i: c for i, c in enumerate([c for c in able if topo.chip(c) == chip[r]])}
        way["far"] = [c for c in able if topo.mates(topo.chip(c), topo.chip(d)) and topo.same_plane(topo.chip(c), chip[r])][0]
        way["mate"], way[None] = cores[partner[r]], None
        full, low = topo.mask(me, cores[partner[r]]), topo.mask(me, d)
        engines = {"low": low, "high": full & ~low}
        pieces[r] = [(k, a, b, way[v], engines[m]) for k, a, b, v, m in (DIRECT if direct else RELAYED)]
    return cores, wid, partner, dest, pieces


def rank_program(g, core, T, topo):
    cores, wid, partner, dest, pieces = plan(T, topo)
    sem = T.sem
    nsent = [0]

    def send(dst, out, src, arrived, mask):
        rid, pid, _ = topo.addr(dst)
        g.remote_dma(out_ap=out, in_ap=src, remote_sem=arrived, local_sem=sem.sent, pid=pid, routing_id=rid, dma_engine_mask=mask)
        nsent[0] += count(mask)

    def codes(buf, a, b):
        return buf[:, a:b].bitcast(dt.uint8)

    def view(k, q, s, a, b):
        return codes(q, a, b) if k == "c" else s[:, a:b]

    def relay_for(r, q, arrived):
        for i, (k, a, b, via, m) in enumerate(pieces[r]):
            if via == core:
                g.wait_ge(sem[arrived % i], count(m))
                d = cores[dest[r]]
                mask = topo.mask(core, d)
                send(d, view(k, T.fq, T.fs, a, b), view(k, q, T.fs, a, b), sem["p%d" % i], mask)

    rank = T.rank_of(core)
    if rank is None:
        for r in pieces:
            relay_for(r, T.fq, "p%d")
        if nsent[0]:
            g.wait_ge(sem.sent, nsent[0])
        return

    low = topo.mask(core, [c for c in cores if topo.chip(c) != topo.chip(core)][0])
    mate = partner[rank]
    po, pp = wid[rank], wid[mate]
    pair = topo.mask(core, cores[mate])

    def load(queue, s, out, in_):
        queue.dma_start(out=out, in_=in_).then_inc(s, 16)

    load(g.sync, sem.l0, T.wb[:, 0:256], T.w1[:, 0:256])
    load(g.scalar, sem.l0, T.wb[:, 256:512], T.w1[:, 256:512])
    load(g.sync, sem.l2, T.wb[:, 4 * W2COL:4 * W2COL + 512], T.w2[:])
    load(g.scalar, sem.l1, T.wb[:, 512:1024], T.w1[:, 512:1024])
    load(g.scalar, sem.l3, T.wb[:, 4 * TCOL[2]:4 * TCOL[2] + 1024], T.w1[:, 1024:2048])
    load(g.scalar, sem.l5, T.xb[:, 0:4 * po], T.x[:, 0:4 * po])

    def quant_w(c):
        g.vector.quantize_mx(T.wq[:, c:c + 128], T.ws[:, c:c + 128], T.wb[:, 4 * c:4 * c + 512]).then_inc(sem.qin, 1)

    g.vector.wait_ge(sem.l0, 32)
    quant_w(TCOL[0])
    g.vector.wait_ge(sem.l1, 16)
    quant_w(TCOL[1])
    g.vector.wait_ge(sem.l2, 16)
    quant_w(W2COL)
    g.vector.wait_ge(sem.l3, 16)
    quant_w(TCOL[2])
    quant_w(TCOL[3])
    g.vector.wait_ge(sem.l5, 16)
    g.vector.quantize_mx(T.xq[:, pp:pp + po], T.xs[:, pp:pp + po], T.xb[:, 0:4 * po]).then_inc(sem.qin, 1)

    xmask = pair & ~low

    def send_tokens():
        g.wait_ge(sem.qin, 6)
        send(cores[mate], codes(T.xq, 0, po), codes(T.xq, pp, pp + po), sem.xarr, xmask)
        send(cores[mate], T.xs[:, 0:po], T.xs[:, pp:pp + po], sem.xarr, xmask)

    xpos = min(XPOS[topo.may_write(core, cores[dest[rank]])], len(pieces[rank]))
    for i, (k, a, b, via, m) in enumerate(pieces[rank]):
        if i == xpos:
            send_tokens()
        g.wait_ge(sem.qin, b // 128)
        to_mate = via == cores[mate]
        send(cores[dest[rank]] if via is None else via, view(k, T.mq if to_mate else T.fq, T.fs, a, b),
             view(k, T.wq, T.ws, a, b), sem[("m%d" if to_mate else "p%d") % i], m)
    if xpos == len(pieces[rank]):
        send_tokens()
    relay_for(mate, T.mq, "m%d")
    g.wait_ge(sem.yc, 1)
    send(cores[mate], T.yland[:, 0:pp], T.ysend[:, 0:pp], sem.yarr, pair)
    g.wait_ge(sem.sent, nsent[0])

    blocks = [
        (T.wq, T.ws, pp, po, 0, 0),
        (T.wq, T.ws, 0, pp, po, 1),
        (T.fq, T.fs, 0, pp, XCOLS, 1),
        (T.fq, T.fs, pp, po, XCOLS + pp, 0),
    ]
    def first(j, t):
        wq, ws, xc, n, hc, yb = blocks[j]
        k, c = 4 * j + t, TCOL[t]
        bank = 512 * (k % NBANK)
        if k >= NBANK:
            o = k - NBANK
            g.tensor.wait_ge(sem.ea if o % 2 == 0 else sem.ev, o // 2 + 1)
        g.tensor.matmul_mx(T.z[:, bank:bank + n], wq[:, c:c + 128], ws[:, c:c + 128], T.xq[:, xc:xc + n], T.xs[:, xc:xc + n],
                           True, True).then_inc(sem.mz, 1)

    def second(j):
        wq, ws, xc, n, hc, yb = blocks[j]
        g.tensor.wait_ge(sem.qh, j + 1)
        g.tensor.matmul_mx(T.yps[:, 512 * yb:512 * yb + n], wq[:, W2COL:W2COL + 128], ws[:, W2COL:W2COL + 128],
                           T.hq[:, hc:hc + n], T.hs[:, hc:hc + n], j < 2, j >= 2).then_inc(sem.my, 1)

    source = [r for r in dest if dest[r] == rank][0]
    waited = []

    def need(c):
        for i, (k, a, b, via, m) in enumerate(pieces[source]):
            if i not in waited and a < c + 128 and b > c:
                waited.append(i)
                last = cores[source] if via is None else via
                g.tensor.wait_ge(sem["p%d" % i], count(topo.mask(last, core)))

    g.tensor.wait_ge(sem.qin, 6)
    for e in SEQ:
        if e == (1, 0):
            g.tensor.wait_ge(sem.xarr, 2 * count(xmask))
        if e in (0, 1, 2, 3):
            if e == 2:
                need(W2COL)
            second(e)
        else:
            if e[0] >= 2:
                need(TCOL[e[1]])
            first(e[0], e[1])

    def evac(k):
        wq, ws, xc, n, hc, yb = blocks[k // 4]
        b, bank = k % 4, 512 * (k % NBANK)
        out, in_ = T.h[:, 4 * hc + b:4 * (hc + n):4], T.z[:, bank:bank + n]
        if k % 2 == 0:
            g.scalar.wait_ge(sem.mz, k + 1)
            g.scalar.activation(out, in_, ActivationFunctionType.Relu, scale=0.041).then_inc(sem.ea, 1)
        else:
            g.vector.wait_ge(sem.mz, k + 1)
            g.vector.tensor_scalar(out, in_, 0.0, 0.041, AluOpType.max, AluOpType.mult).then_inc(sem.ev, 1)

    for j in range(4):
        wq, ws, xc, n, hc, yb = blocks[j]
        for b in range(4):
            evac(4 * j + b)
        g.vector.wait_ge(sem.ea, 2 * j + 2)
        g.vector.wait_ge(sem.ev, 2 * j + 2)
        g.vector.quantize_mx(T.hq[:, hc:hc + n], T.hs[:, hc:hc + n], T.h[:, 4 * hc:4 * (hc + n)]).then_inc(sem.qh, 1)
        if j == 2:
            g.vector.wait_ge(sem.my, 3)
            g.vector.tensor_copy(T.ysend[:, 0:pp], T.yps[:, 512:512 + pp]).then_inc(sem.yc, 1)

    g.vector.wait_ge(sem.my, 4)
    g.vector.wait_ge(sem.yarr, count(pair))
    g.vector.tensor_tensor(T.yout[:, 0:po], T.yps[:, 0:po], T.yland[:, 0:po], AluOpType.add).then_inc(sem.fin, 1)
    g.sync.wait_ge(sem.fin, 1)
    g.sync.dma_start(out=T.y[:, 0:po], in_=T.yout[:, 0:po]).then_inc(sem.st, 16)
    g.sync.wait_ge(sem.st, 16)
